import numpy as np
import ml_dtypes


def mxq(x, axis, fmt="e4m3"):
    dtype, down = {"e4m3": (ml_dtypes.float8_e4m3fn, 7), "e5m2": (ml_dtypes.float8_e5m2, 14)}[fmt]
    v = np.moveaxis(np.asarray(x, np.float32).astype(ml_dtypes.bfloat16).astype(np.float64), axis, -1)
    blocks = v.reshape(v.shape[:-1] + (-1, 32))
    amax = np.abs(blocks).max(-1, keepdims=True)
    byte = np.maximum(np.where(amax > 0, np.frexp(amax)[1] - 1 + 127, 0) - down, 1)
    scale = np.exp2(byte - 127.0)
    codes = (blocks / scale).astype(np.float32).astype(dtype).astype(np.float64)
    return np.moveaxis((codes * scale).reshape(v.shape), -1, axis)


WIDE = False


def mx_kscale(k):
    if not WIDE:
        return np.ones(k)
    levels = np.array([10, -10, 5, -5, 0])
    if k % 512:
        return np.exp2(np.random.permutation(np.resize(levels, k // 32))).repeat(32)
    a = np.empty((k // 512, 16))
    for p in range(k // 512):
        a[p, :8] = np.random.permutation(np.resize(levels, 8))
        for g in range(8):
            far = levels[np.abs(levels - a[p, g]) >= 10]
            a[p, g + 8] = far[np.random.randint(len(far))]
    return np.exp2(a.ravel()).repeat(32)


def f64(x):
    return np.asarray(x).astype(np.float64)


def striped(idx):
    return np.tile(idx.reshape(-1, 16).T, (8, 1)).astype(np.uint16)


def unstriped(offs):
    return offs[:16].T.reshape(-1).astype(np.int64)


E2M1 = np.array([0.0, 0.5, 1.0, 1.5, 2.0, 3.0, 4.0, 6.0, -0.0, -0.5, -1.0, -1.5, -2.0, -3.0, -4.0, -6.0])


def pack_weight(w, fmt):
    k, n = w.shape
    w = f64(np.asarray(w, np.float32).astype(ml_dtypes.bfloat16)).reshape(k // 32, 32, n)
    amax = np.abs(w).max(1)
    if fmt == "e4m3":
        byte = np.frexp(amax)[1] - 1 + 127 - 7
    else:
        mant, ex = np.frexp(amax / 6.0)
        byte = np.where(mant > 0.5, ex, ex - 1) + 127
    byte = np.clip(np.where(amax > 0, byte, 1), 1, 254)
    scaled = (w * np.exp2(127.0 - byte)[:, None, :]).reshape(k, n).astype(np.float32)
    by_word = np.ascontiguousarray(scaled.reshape(k // 512, 128, 4, n).transpose(0, 1, 3, 2))
    if fmt == "e4m3":
        words = by_word.astype(ml_dtypes.float8_e4m3fn).view(np.uint8)
    else:
        c = by_word.astype(ml_dtypes.float4_e2m1fn).view(np.uint8) & 0xF
        words = (c[..., 0::2] | (c[..., 1::2] << 4)).reshape(k // 512, 128, 2 * n)
    return np.ascontiguousarray(words), np.ascontiguousarray(byte.astype(np.uint8).reshape(k // 512, 16, n))


def unpack_weight(words, scales, fmt):
    g, _, n = scales.shape
    words = np.ascontiguousarray(words).reshape(g, 128, n, -1)
    if fmt == "e4m3":
        vals = words.view(ml_dtypes.float8_e4m3fn).astype(np.float64)
    else:
        nib = np.empty((g, 128, n, 4), np.uint8)
        nib[..., 0::2] = words & 0xF
        nib[..., 1::2] = words >> 4
        vals = E2M1[nib]
    vals = vals * np.repeat(np.exp2(scales.astype(np.float64) - 127.0), 8, axis=1)[..., None]
    return vals.transpose(0, 1, 3, 2).reshape(g * 512, n)


def gelu(v):
    return 0.5 * v * (1.0 + np.tanh(np.sqrt(2.0 / np.pi) * (v + 0.044715 * v**3)))


def bf(x):
    return np.asarray(x, np.float32).astype(ml_dtypes.bfloat16)


def planes(Y):
    n, m = Y.shape
    b = f64(bf(Y)).reshape(n // 32, 32, m)
    amax = np.abs(b).max(1)
    byte = np.clip(np.where(amax > 0, np.frexp(amax)[1] - 1 + 127 - 7, 1), 1, 254)
    codes = (b * np.exp2(127.0 - byte)[:, None, :]).reshape(n, m).astype(np.float32).astype(ml_dtypes.float8_e4m3fn).view(np.uint8)
    words = codes.reshape(n // 512, 128, 4, m).transpose(0, 1, 3, 2)
    return np.ascontiguousarray(words), np.ascontiguousarray(byte.astype(np.uint8).reshape(n // 512, 16, m))


K, T, S, H, T2, P, N = 1024, 4096, 1024, 512, 2048, 1024, 1024

def setup_inputs():
    n = np.random.standard_normal
    s, u = mx_kscale(K)[:, None], mx_kscale(H)[:, None]
    rs = np.exp(0.8 * n(N))
    tab_words, tab_scales = pack_weight(n((K, T)) * s, "e4m3")
    w2_words, w2_scales = pack_weight(2.0 * n((K, H)) / np.sqrt(K) / s, "e2m1")
    w3_words, w3_scales = pack_weight(n((H, N)) * rs / np.sqrt(H) / u, "e4m3")
    return {
        "tab_words": tab_words, "tab_scales": tab_scales,
        "offs": striped(np.random.permutation(T)[:S]),
        "w1": (n((K, H)) / np.sqrt(K) / s).astype(np.float32),
        "w2_words": w2_words, "w2_scales": w2_scales,
        "gain": (np.random.uniform(0.8, 1.6, H) * u[:, 0]).astype(np.float32),
        "page0": (n((H, T2)) * u).astype(np.float32),
        "wgs": np.exp(0.3 * n((128, S))).astype(np.float32),
        "offs2": striped(np.random.permutation(T2)[:S]),
        "offs3": striped(np.random.permutation(T2)[:P]),
        "offs4": striped(np.random.permutation(T2)[:P]),
        "keep": np.random.uniform(0.4, 1.1, H).astype(np.float32),
        "w3_words": w3_words, "w3_scales": w3_scales,
        "b3": (0.5 * n(N) * rs).astype(np.float32),
    }

def reference(tab_words, tab_scales, offs, w1, w2_words, w2_scales, gain, page0, wgs, offs2, offs3, offs4, keep, w3_words, w3_scales, b3):
    v = unpack_weight(tab_words, tab_scales, "e4m3")[:, unstriped(offs)]
    flat = mxq(f64(w1), 0, "e4m3").T @ v
    bent = np.tanh(unpack_weight(w2_words, w2_scales, "e2m1").T @ v)
    h = f64(gain)[:, None] * (flat + bent)
    before = f64(page0)
    page = before.copy()
    page[:, unstriped(offs2)] = np.tile(f64(wgs), (H // 128, 1)) * h
    x = page[:, unstriped(offs3)] - f64(keep)[:, None] * before[:, unstriped(offs4)]
    xq = mxq(x, 0, "e4m3")
    w3 = unpack_weight(w3_words, w3_scales, "e4m3")
    y = (w3.T @ xq) + f64(b3)[:, None]
    words, scales = planes(y)
    return y, words, scales

@@ -1,0 +1,289 @@
+from contextlib import ExitStack
+
+import concourse.mybir as mybir
+from concourse.masks import make_identity
+
+K, T, S, H, T2, M, N = 1024, 4096, 1024, 512, 2048, 1024, 1024
+FLOPS = 2 * (2 * K * H * S + H * N * M)
+
+F32 = mybir.dt.float32
+BF16 = mybir.dt.bfloat16
+I32 = mybir.dt.int32
+U32 = mybir.dt.uint32
+U16 = mybir.dt.uint16
+U8 = mybir.dt.uint8
+FP8X4 = mybir.dt.float8_e4m3fn_x4
+FP4X4 = mybir.dt.float4_e2m1fn_x4
+ACT = mybir.ActivationFunctionType
+MULT = mybir.AluOpType.mult
+SUB = mybir.AluOpType.subtract
+ADD = mybir.AluOpType.add
+
+P = 128
+PACK = 4
+PASSES = K // (P * PACK)
+HALF = 512
+JS = 256
+M_SLICES = [(0, 128), (128, 256), (384, 256), (640, 256), (896, 128)]
+MW = 256
+
+
+def cols(start, width):
+    return slice(start // 16, (start + width) // 16)
+
+
+def tile_list_calving_front_retreat_kernel(
+    tc, tab_words, tab_scales, offs, w1, w2_words, w2_scales, gain, page0, wgs, offs2, offs3, offs4, keep,
+    w3_words, w3_scales, b3, out_0, out_1, out_2,
+):
+    nc = tc.nc
+    with ExitStack() as ctx:
+        held = ctx.enter_context(tc.tile_pool(name="held", bufs=1))
+        ring = ctx.enter_context(tc.tile_pool(name="ring", bufs=2))
+        shared = ctx.enter_context(tc.tile_pool(name="shared", bufs=1))
+        psum = ctx.enter_context(tc.psum_pool(name="psum", bufs=4))
+
+        def plane_rows(dst, src):
+            for r in range(4):
+                nc.sync.dma_start(
+                    out=dst[:].bitcast(I32)[r:P:32, :, :],
+                    in_=src[:, r:16:4, :].bitcast(I32).rearrange("a q c -> q a c"),
+                )
+
+        list1 = held.tile([P, S // 16], U16, name="list1")
+        list2 = held.tile([P, S // 16], U16, name="list2")
+        list3 = held.tile([P, M // 16], U16, name="list3")
+        list4 = held.tile([P, M // 16], U16, name="list4")
+        nc.sync.dma_start(list1[:], offs)
+
+        def load_w1(a):
+            raw = ring.tile([P, PACK, H], F32, name="w1_raw", tag="wide")
+            nc.sync.dma_start(out=raw[:], in_=w1[a * 512:(a + 1) * 512, :].rearrange("(p i) r -> p i r", i=PACK))
+            return raw
+
+        tab_s = held.tile([P, PASSES, T], U8, name="tab_s")
+        w2_s = held.tile([P, PASSES, H], U8, name="w2_s", align_bytes=64)
+        v_s = held.tile([P, PASSES, S], U8, name="v_s", align_bytes=64)
+        w3_s_raw = held.tile([P, 1, N], U8, name="w3_s_raw")
+        nc.vector.memset(tab_s[:, 0, :].bitcast(I32), 0)
+        nc.gpsimd.memset(tab_s[:, 1, :].bitcast(I32), 0)
+        nc.vector.memset(w2_s[:].bitcast(I32), 0)
+        nc.vector.memset(v_s[:].bitcast(I32), 0)
+        nc.vector.memset(w3_s_raw[:].bitcast(I32), 0)
+        ident = held.tile([P, P], F32, name="ident")
+        make_identity(nc, ident[:])
+        w1_raw = [load_w1(0)]
+        nc.sync.dma_start(
+            out=tab_s[:].bitcast(I32)[0:P:8, :, :], in_=tab_scales.bitcast(I32).rearrange("a q c -> q a c")
+        )
+        picked_s = held.tile([P, PASSES, S], U8, name="picked_s")
+        for a in range(PASSES):
+            nc.vector.tensor_copy(picked_s[:, a, :], tab_s[:, a, :].indirect(list1[:]))
+        for r in range(4):
+            nc.gpsimd.dma_start(
+                out=v_s[:].bitcast(I32)[r:P:32, :, :], in_=picked_s[:].bitcast(I32)[8 * r:P:32, :, :]
+            )
+        w1_raw.append(load_w1(1))
+        w2_w = held.tile([P, PASSES, 2 * H], U8, name="w2_w", align_bytes=64)
+        nc.sync.dma_start(out=w2_w[:].bitcast(I32), in_=w2_words.bitcast(I32).rearrange("a p c -> p a c"))
+        tab_w = [held.tile([P, T], I32, name="tab_w0"), shared.tile([P, T], I32, name="tab_w1", offset=0)]
+        nc.sync.dma_start(out=tab_w[0][:], in_=tab_words[0].rearrange("p n i -> p (n i)").bitcast(I32))
+        plane_rows(w2_s, w2_scales)
+        nc.sync.dma_start(out=tab_w[1][:], in_=tab_words[1].rearrange("p n i -> p (n i)").bitcast(I32))
+        keep_t = held.tile([P, PACK], F32, name="keep_t")
+        nc.sync.dma_start(out=keep_t[:], in_=keep.rearrange("(p t) -> p t", t=PACK))
+        nc.sync.dma_start(list4[:], offs4)
+
+        page_rows = page0.rearrange("(p t) c -> t p c", t=PACK)
+        page = [held.tile([P, T2], F32, name=f"page{t}") for t in range(PACK)]
+        before = [page[0]] + [held.tile([P, T2], F32, name=f"before{t}") for t in range(1, PACK)]
+        wgs_rows = wgs.rearrange("(q t) j -> q t j", t=PACK)
+        wg = {}
+
+        def load_wg(u, half):
+            tile = held.tile([P, 2, HALF], F32, name=f"wg{u}{half}")
+            for quad in range(4):
+                nc.sync.dma_start(
+                    out=tile[32 * quad:32 * quad + 32, :, :],
+                    in_=wgs_rows[:, 2 * u:2 * u + 2, half * HALF:(half + 1) * HALF],
+                )
+            wg[u, half] = tile
+
+        w3_raw = held.tile([P, N], I32, name="w3_raw")
+        b3_t = held.tile([P, 2, PACK], F32, name="b3_t")
+        nc.sync.dma_start(out=page[0][:], in_=page_rows[0])
+        gain_t = held.tile([P, PACK], F32, name="gain_t")
+        nc.sync.dma_start(out=gain_t[:], in_=gain.rearrange("(p t) -> p t", t=PACK))
+        nc.sync.dma_start(list2[:], offs2)
+        nc.sync.dma_start(out=w3_raw[:], in_=w3_words[0].rearrange("p n i -> p (n i)").bitcast(I32))
+        plane_rows(w3_s_raw, w3_scales)
+        load_wg(0, 0)
+        nc.sync.dma_start(out=page[1][:], in_=page_rows[1])
+        load_wg(0, 1)
+        nc.sync.dma_start(out=page[2][:], in_=page_rows[2])
+        load_wg(1, 0)
+        nc.sync.dma_start(out=page[3][:], in_=page_rows[3])
+        load_wg(1, 1)
+        nc.sync.dma_start(list3[:], offs3)
+        nc.sync.dma_start(out=b3_t[:], in_=b3.rearrange("(g p t) -> p g t", g=2, t=PACK))
+        for t in range(1, PACK):
+            nc.sync.dma_start(out=before[t][:], in_=page_rows[t])
+
+        w1_c, w1_s = [], []
+        for a in range(PASSES):
+            grouped = ring.tile([P, H, PACK], BF16, name="w1_grouped", align_bytes=64)
+            nc.scalar.copy(out=grouped[:], in_=w1_raw[a][:].rearrange("p i r -> p r i"))
+            codes = held.tile([P, H], U32, name=f"w1_c{a}", align_bytes=64)
+            scales = held.tile([P, H], U8, name=f"w1_s{a}", align_bytes=64)
+            nc.vector.quantize_mx(
+                out=codes[:].bitcast(FP8X4), scales=scales[:], in_=grouped[:].rearrange("p r i -> p (r i)")
+            )
+            w1_c.append(codes)
+            w1_s.append(scales)
+
+        keep_wide = held.tile([P, PACK, MW], F32, name="keep_wide")
+        for t in range(PACK):
+            nc.vector.tensor_copy(keep_wide[:, t, :], keep_t[:, t:t + 1].to_broadcast([P, MW]))
+
+        v_w = {}
+        for a in range(PASSES):
+            for half in range(S // HALF):
+                picked = held.tile([P, HALF], U32, name=f"v_w{a}{half}", align_bytes=64)
+                nc.vector.tensor_copy(
+                    picked[:], tab_w[a][:].bitcast(U32).indirect(list1[:, cols(half * HALF, HALF)])
+                )
+                v_w[a, half] = picked
+
+        kept0 = shared.tile([P, M], F32, name="kept0", offset=0)
+        for m0 in range(0, M, MW):
+            nc.vector.tensor_tensor(
+                kept0[:, m0:m0 + MW], page[0][:].indirect(list4[:, cols(m0, MW)]), keep_wide[:, 0, :], MULT
+            )
+
+        w3_w = shared.tile([P, N], I32, name="w3_w", align_bytes=64, offset=4 * M)
+        w3_s = shared.tile([P, N], U8, name="w3_s", align_bytes=64, offset=4 * M + 4 * N)
+        nc.vector.tensor_copy(
+            out=w3_w[:].rearrange("p (g t q) -> p g q t", g=2, t=PACK),
+            in_=w3_raw[:].rearrange("p (g q t) -> p g q t", g=2, t=PACK),
+        )
+        nc.vector.tensor_copy(
+            out=w3_s[:].rearrange("p (g t q) -> p g q t", g=2, t=PACK),
+            in_=w3_s_raw[:, 0, :].rearrange("p (g q t) -> p g q t", g=2, t=PACK),
+        )
+
+        for j0 in range(0, S, JS):
+            sums = [psum.tile([P, 2, JS], F32, name="sums", tag="turn") for u in range(2)]
+            parts = []
+            for jb in range(JS // P):
+                j = j0 + jb * P
+                half, c0 = divmod(j, HALF)
+                flat = psum.tile([P, H], F32, name="flat", tag="prod")
+                bent = psum.tile([P, H], F32, name="bent", tag="prod")
+                for a in range(PASSES):
+                    nc.tensor.matmul_mx(
+                        out=bent[:],
+                        lhsT=v_w[a, half][:, c0:c0 + P].bitcast(FP8X4), lhsT_scale=v_s[:, a, j:j + P],
+                        rhs=w2_w[:, a, :].bitcast(FP4X4), rhs_scale=w2_s[:, a, :],
+                        start=(a == 0), stop=(a == PASSES - 1),
+                    )
+                    nc.tensor.matmul_mx(
+                        out=flat[:],
+                        lhsT=v_w[a, half][:, c0:c0 + P].bitcast(FP8X4), lhsT_scale=v_s[:, a, j:j + P],
+                        rhs=w1_c[a][:].bitcast(FP8X4), rhs_scale=w1_s[a][:],
+                        start=(a == 0), stop=(a == PASSES - 1),
+                    )
+                bent_sb = ring.tile([P, PACK, P], F32, name="bent_sb", bufs=3)
+                flat_sb = ring.tile([P, PACK, P], F32, name="flat_sb", bufs=3)
+                nc.scalar.activation(out=bent_sb[:], in_=bent[:].rearrange("j (p t) -> j t p", t=PACK), func=ACT.Tanh)
+                nc.scalar.copy(out=flat_sb[:], in_=flat[:].rearrange("j (p t) -> j t p", t=PACK))
+                parts.append((bent_sb, flat_sb))
+            for t in range(PACK):
+                for jb, (bent_sb, flat_sb) in enumerate(parts):
+                    dst = sums[t // 2][:, t % 2, jb * P:(jb + 1) * P]
+                    nc.tensor.matmul(dst, lhsT=bent_sb[:, t, :], rhs=ident[:], start=True, stop=False, is_transpose=True)
+                    nc.tensor.matmul(dst, lhsT=flat_sb[:, t, :], rhs=ident[:], start=False, stop=True, is_transpose=True)
+            half, c0 = divmod(j0, HALF)
+            for t in range(PACK):
+                h = ring.tile([P, JS], F32, name="h", bufs=8)
+                nc.scalar.activation(out=h[:], in_=sums[t // 2][:, t % 2, :], func=ACT.Copy, scale=gain_t[:, t:t + 1])
+                nc.vector.tensor_tensor(
+                    page[t][:].indirect(list2[:, cols(j0, JS)]), h[:], wg[t // 2, half][:, t % 2, c0:c0 + JS], MULT
+                )
+
+        y_s = held.tile([P, 2, M], U8, name="y_s", align_bytes=64)
+        words_out = out_1.rearrange("g p m t -> p g (m t)").bitcast(I32)
+
+        def gather_x(m0, w):
+            kept = ring.tile([P, PACK - 1, MW], F32, name="kept", bufs=1)
+            for t in range(1, PACK):
+                nc.vector.tensor_tensor(
+                    kept[:, t - 1, :w], before[t][:].indirect(list4[:, cols(m0, w)]), keep_wide[:, t, :w], MULT
+                )
+            x = ring.tile([P, PACK, w], F32, name="x", bufs=1)
+            for t in range(PACK):
+                old = kept0[:, m0:m0 + w] if t == 0 else kept[:, t - 1, :w]
+                nc.vector.tensor_tensor(x[:, t, :], page[t][:].indirect(list3[:, cols(m0, w)]), old, SUB)
+            x_grouped = ring.tile([P, w, PACK], BF16, name="x_grouped", align_bytes=64)
+            nc.scalar.copy(out=x_grouped[:], in_=x[:].rearrange("p t m -> p m t"))
+            x_c = ring.tile([P, w], U32, name="x_c", align_bytes=64)
+            x_s = ring.tile([P, w], U8, name="x_s", align_bytes=64)
+            nc.vector.quantize_mx(
+                out=x_c[:].bitcast(FP8X4), scales=x_s[:], in_=x_grouped[:].rearrange("p m t -> p (m t)")
+            )
+            return x_c, x_s
+
+        def multiply(index, x_c, x_s):
+            m0, w = M_SLICES[index]
+            per_bank = 512 // w
+            y = ring.tile([P, 2, PACK, w], F32, name="y", tag="wide")
+            for g in range(2):
+                for t0 in range(0, PACK, per_bank):
+                    bank = psum.tile([P, per_bank, w], F32, name="bank", tag=("prod", "turn")[index % 2])
+                    for tt in range(per_bank):
+                        c0 = (g * PACK + t0 + tt) * P
+                        nc.tensor.matmul_mx(
+                            out=bank[:, tt, :],
+                            lhsT=w3_w[:, c0:c0 + P].bitcast(FP8X4), lhsT_scale=w3_s[:, c0:c0 + P],
+                            rhs=x_c[:].bitcast(FP8X4), rhs_scale=x_s[:],
+                            start=True, stop=True,
+                        )
+                    if index == len(M_SLICES) - 1 and g == 0:
+                        bias = b3_t[:, g, t0:t0 + per_bank].unsqueeze(2).to_broadcast([P, per_bank, w])
+                        nc.vector.tensor_tensor(y[:, g, t0:t0 + per_bank, :], bank[:], bias, ADD)
+                    else:
+                        for tt in range(per_bank):
+                            t = t0 + tt
+                            nc.scalar.activation(
+                                out=y[:, g, t, :], in_=bank[:, tt, :], func=ACT.Identity, bias=b3_t[:, g, t:t + 1]
+                            )
+                nc.sync.dma_start(
+                    out=out_0[g * 512:(g + 1) * 512, m0:m0 + w].rearrange("(p t) m -> p t m", t=PACK), in_=y[:, g, :, :]
+                )
+            return y
+
+        def planes(index, y):
+            m0, w = M_SLICES[index]
+            y_c = held.tile([P, 2, w], I32, name=f"y_c{index}", align_bytes=64)
+            for g in range(2):
+                y_grouped = ring.tile([P, w, PACK], BF16, name=f"y_grouped{g}", align_bytes=64)
+                if g == 0:
+                    nc.vector.tensor_copy(out=y_grouped[:], in_=y[:, g, :, :].rearrange("p t m -> p m t"))
+                else:
+                    nc.scalar.copy(out=y_grouped[:], in_=y[:, g, :, :].rearrange("p t m -> p m t"))
+                nc.vector.quantize_mx(
+                    out=y_c[:, g, :].bitcast(FP8X4), scales=y_s[:, g, m0:m0 + w],
+                    in_=y_grouped[:].rearrange("p m t -> p (m t)"),
+                )
+            nc.sync.dma_start(out=words_out[:, :, m0:m0 + w], in_=y_c[:])
+
+        quantised = gather_x(*M_SLICES[0])
+        for index in range(len(M_SLICES)):
+            y = multiply(index, *quantised)
+            if index + 1 < len(M_SLICES):
+                quantised = gather_x(*M_SLICES[index + 1])
+            planes(index, y)
+        for r in range(4):
+            nc.scalar.dma_start(
+                out=out_2[:, r:16:4, :].bitcast(I32).rearrange("g q m -> q g m"),
+                in_=y_s[:].bitcast(I32)[r:P:32, :, :],
+            )

@@ -45,10 +45,13 @@ def tile_list_calving_front_retreat_kernel(
 
         def plane_rows(dst, src):
             for r in range(4):
-                nc.sync.dma_start(
+                nc.gpsimd.dma_start(
                     out=dst[:].bitcast(I32)[r:P:32, :, :],
                     in_=src[:, r:16:4, :].bitcast(I32).rearrange("a q c -> q a c"),
                 )
+
+        def interleave(copy, dst, src):
+            copy(out=dst.rearrange("p (c i) t -> p c t i", i=4), in_=src.rearrange("p t (c i) -> p c t i", i=4))
 
         list1 = held.tile([P, S // 16], U16, name="list1")
         list2 = held.tile([P, S // 16], U16, name="list2")
@@ -65,33 +68,33 @@ def tile_list_calving_front_retreat_kernel(
         w2_s = held.tile([P, PASSES, H], U8, name="w2_s", align_bytes=64)
         v_s = held.tile([P, PASSES, S], U8, name="v_s", align_bytes=64)
         w3_s_raw = held.tile([P, 1, N], U8, name="w3_s_raw")
-        nc.vector.memset(tab_s[:, 0, :].bitcast(I32), 0)
-        nc.gpsimd.memset(tab_s[:, 1, :].bitcast(I32), 0)
-        nc.vector.memset(w2_s[:].bitcast(I32), 0)
+        nc.vector.memset(tab_s[:].bitcast(I32), 0)
+        nc.gpsimd.memset(w2_s[:].bitcast(I32), 0)
         nc.vector.memset(v_s[:].bitcast(I32), 0)
         nc.vector.memset(w3_s_raw[:].bitcast(I32), 0)
         ident = held.tile([P, P], F32, name="ident")
         make_identity(nc, ident[:])
+        warm = held.tile([P, 1], F32, name="warm")
+        nc.scalar.activation(out=warm[:], in_=ident[:, 0:1], func=ACT.Tanh)
+        plane_rows(w2_s, w2_scales)
+        keep_t = held.tile([P, PACK], F32, name="keep_t")
+        nc.gpsimd.dma_start(out=keep_t[:], in_=keep.rearrange("(p t) -> p t", t=PACK))
+        gain_t = held.tile([P, PACK], F32, name="gain_t")
+        nc.gpsimd.dma_start(out=gain_t[:], in_=gain.rearrange("(p t) -> p t", t=PACK))
+        plane_rows(w3_s_raw, w3_scales)
+        b3_t = held.tile([P, 2, PACK], F32, name="b3_t")
+        nc.gpsimd.dma_start(out=b3_t[:], in_=b3.rearrange("(g p t) -> p g t", g=2, t=PACK))
+
         w1_raw = [load_w1(0)]
         nc.sync.dma_start(
             out=tab_s[:].bitcast(I32)[0:P:8, :, :], in_=tab_scales.bitcast(I32).rearrange("a q c -> q a c")
         )
-        picked_s = held.tile([P, PASSES, S], U8, name="picked_s")
-        for a in range(PASSES):
-            nc.vector.tensor_copy(picked_s[:, a, :], tab_s[:, a, :].indirect(list1[:]))
-        for r in range(4):
-            nc.gpsimd.dma_start(
-                out=v_s[:].bitcast(I32)[r:P:32, :, :], in_=picked_s[:].bitcast(I32)[8 * r:P:32, :, :]
-            )
         w1_raw.append(load_w1(1))
         w2_w = held.tile([P, PASSES, 2 * H], U8, name="w2_w", align_bytes=64)
         nc.sync.dma_start(out=w2_w[:].bitcast(I32), in_=w2_words.bitcast(I32).rearrange("a p c -> p a c"))
         tab_w = [held.tile([P, T], I32, name="tab_w0"), shared.tile([P, T], I32, name="tab_w1", offset=0)]
-        nc.sync.dma_start(out=tab_w[0][:], in_=tab_words[0].rearrange("p n i -> p (n i)").bitcast(I32))
-        plane_rows(w2_s, w2_scales)
-        nc.sync.dma_start(out=tab_w[1][:], in_=tab_words[1].rearrange("p n i -> p (n i)").bitcast(I32))
-        keep_t = held.tile([P, PACK], F32, name="keep_t")
-        nc.sync.dma_start(out=keep_t[:], in_=keep.rearrange("(p t) -> p t", t=PACK))
+        for a in range(PASSES):
+            nc.sync.dma_start(out=tab_w[a][:], in_=tab_words[a].rearrange("p n i -> p (n i)").bitcast(I32))
         nc.sync.dma_start(list4[:], offs4)
 
         page_rows = page0.rearrange("(p t) c -> t p c", t=PACK)
@@ -110,29 +113,31 @@ def tile_list_calving_front_retreat_kernel(
             wg[u, half] = tile
 
         w3_raw = held.tile([P, N], I32, name="w3_raw")
-        b3_t = held.tile([P, 2, PACK], F32, name="b3_t")
         nc.sync.dma_start(out=page[0][:], in_=page_rows[0])
-        gain_t = held.tile([P, PACK], F32, name="gain_t")
-        nc.sync.dma_start(out=gain_t[:], in_=gain.rearrange("(p t) -> p t", t=PACK))
-        nc.sync.dma_start(list2[:], offs2)
+        picked_s = held.tile([P, PASSES, S], U8, name="picked_s")
+        for a in range(PASSES):
+            nc.vector.tensor_copy(picked_s[:, a, :], tab_s[:, a, :].indirect(list1[:]))
+        for r in range(4):
+            nc.scalar.dma_start(
+                out=v_s[:].bitcast(I32)[r:P:32, :, :], in_=picked_s[:].bitcast(I32)[8 * r:P:32, :, :]
+            )
         nc.sync.dma_start(out=w3_raw[:], in_=w3_words[0].rearrange("p n i -> p (n i)").bitcast(I32))
-        plane_rows(w3_s_raw, w3_scales)
+        nc.sync.dma_start(list2[:], offs2)
         load_wg(0, 0)
         nc.sync.dma_start(out=page[1][:], in_=page_rows[1])
-        load_wg(0, 1)
         nc.sync.dma_start(out=page[2][:], in_=page_rows[2])
         load_wg(1, 0)
+        load_wg(0, 1)
         nc.sync.dma_start(out=page[3][:], in_=page_rows[3])
         load_wg(1, 1)
         nc.sync.dma_start(list3[:], offs3)
-        nc.sync.dma_start(out=b3_t[:], in_=b3.rearrange("(g p t) -> p g t", g=2, t=PACK))
         for t in range(1, PACK):
             nc.sync.dma_start(out=before[t][:], in_=page_rows[t])
 
         w1_c, w1_s = [], []
         for a in range(PASSES):
             grouped = ring.tile([P, H, PACK], BF16, name="w1_grouped", align_bytes=64)
-            nc.scalar.copy(out=grouped[:], in_=w1_raw[a][:].rearrange("p i r -> p r i"))
+            interleave(nc.scalar.copy, grouped[:], w1_raw[a][:])
             codes = held.tile([P, H], U32, name=f"w1_c{a}", align_bytes=64)
             scales = held.tile([P, H], U8, name=f"w1_s{a}", align_bytes=64)
             nc.vector.quantize_mx(
@@ -163,12 +168,12 @@ def tile_list_calving_front_retreat_kernel(
         w3_w = shared.tile([P, N], I32, name="w3_w", align_bytes=64, offset=4 * M)
         w3_s = shared.tile([P, N], U8, name="w3_s", align_bytes=64, offset=4 * M + 4 * N)
         nc.vector.tensor_copy(
-            out=w3_w[:].rearrange("p (g t q) -> p g q t", g=2, t=PACK),
-            in_=w3_raw[:].rearrange("p (g q t) -> p g q t", g=2, t=PACK),
+            out=w3_w[:].rearrange("p (g t c i) -> p g c t i", g=2, t=PACK, i=4),
+            in_=w3_raw[:].rearrange("p (g c i t) -> p g c t i", g=2, t=PACK, i=4),
         )
         nc.vector.tensor_copy(
-            out=w3_s[:].rearrange("p (g t q) -> p g q t", g=2, t=PACK),
-            in_=w3_s_raw[:, 0, :].rearrange("p (g q t) -> p g q t", g=2, t=PACK),
+            out=w3_s[:].rearrange("p (g t c i) -> p g c t i", g=2, t=PACK, i=16),
+            in_=w3_s_raw[:, 0, :].rearrange("p (g c i t) -> p g c t i", g=2, t=PACK, i=16),
         )
 
         for j0 in range(0, S, JS):
@@ -224,7 +229,7 @@ def tile_list_calving_front_retreat_kernel(
                 old = kept0[:, m0:m0 + w] if t == 0 else kept[:, t - 1, :w]
                 nc.vector.tensor_tensor(x[:, t, :], page[t][:].indirect(list3[:, cols(m0, w)]), old, SUB)
             x_grouped = ring.tile([P, w, PACK], BF16, name="x_grouped", align_bytes=64)
-            nc.scalar.copy(out=x_grouped[:], in_=x[:].rearrange("p t m -> p m t"))
+            interleave(nc.scalar.copy, x_grouped[:], x[:])
             x_c = ring.tile([P, w], U32, name="x_c", align_bytes=64)
             x_s = ring.tile([P, w], U8, name="x_s", align_bytes=64)
             nc.vector.quantize_mx(
@@ -266,10 +271,7 @@ def tile_list_calving_front_retreat_kernel(
             y_c = held.tile([P, 2, w], I32, name=f"y_c{index}", align_bytes=64)
             for g in range(2):
                 y_grouped = ring.tile([P, w, PACK], BF16, name=f"y_grouped{g}", align_bytes=64)
-                if g == 0:
-                    nc.vector.tensor_copy(out=y_grouped[:], in_=y[:, g, :, :].rearrange("p t m -> p m t"))
-                else:
-                    nc.scalar.copy(out=y_grouped[:], in_=y[:, g, :, :].rearrange("p t m -> p m t"))
+                interleave((nc.vector.tensor_copy, nc.scalar.copy)[g], y_grouped[:], y[:, g, :, :])
                 nc.vector.quantize_mx(
                     out=y_c[:, g, :].bitcast(FP8X4), scales=y_s[:, g, m0:m0 + w],
                     in_=y_grouped[:].rearrange("p m t -> p (m t)"),

@@ -43,9 +43,9 @@ def tile_list_calving_front_retreat_kernel(
         shared = ctx.enter_context(tc.tile_pool(name="shared", bufs=1))
         psum = ctx.enter_context(tc.psum_pool(name="psum", bufs=4))
 
-        def plane_rows(dst, src):
+        def plane_rows(queue, dst, src):
             for r in range(4):
-                nc.gpsimd.dma_start(
+                queue.dma_start(
                     out=dst[:].bitcast(I32)[r:P:32, :, :],
                     in_=src[:, r:16:4, :].bitcast(I32).rearrange("a q c -> q a c"),
                 )
@@ -68,20 +68,35 @@ def tile_list_calving_front_retreat_kernel(
         w2_s = held.tile([P, PASSES, H], U8, name="w2_s", align_bytes=64)
         v_s = held.tile([P, PASSES, S], U8, name="v_s", align_bytes=64)
         w3_s_raw = held.tile([P, 1, N], U8, name="w3_s_raw")
-        nc.vector.memset(tab_s[:].bitcast(I32), 0)
+        nc.vector.memset(tab_s[:, 0, :].bitcast(I32), 0)
+        nc.gpsimd.memset(w3_s_raw[:].bitcast(I32), 0)
+        nc.vector.memset(tab_s[:, 1, :].bitcast(I32), 0)
         nc.gpsimd.memset(w2_s[:].bitcast(I32), 0)
         nc.vector.memset(v_s[:].bitcast(I32), 0)
-        nc.vector.memset(w3_s_raw[:].bitcast(I32), 0)
         ident = held.tile([P, P], F32, name="ident")
         make_identity(nc, ident[:])
         warm = held.tile([P, 1], F32, name="warm")
         nc.scalar.activation(out=warm[:], in_=ident[:, 0:1], func=ACT.Tanh)
-        plane_rows(w2_s, w2_scales)
+
+        wgs_rows = wgs.rearrange("(q t) j -> q t j", t=PACK)
+        wg = {}
+
+        def load_wg(queue, u, j0, width):
+            tile = held.tile([P, 2, width], F32, name=f"wg{u}_{j0}")
+            for quad in (0, 2, 1, 3):
+                queue.dma_start(
+                    out=tile[32 * quad:32 * quad + 32, :, :], in_=wgs_rows[:, 2 * u:2 * u + 2, j0:j0 + width]
+                )
+            for c0 in range(0, width, JS):
+                for tt in range(2):
+                    wg[2 * u + tt, j0 + c0] = tile[:, tt, c0:c0 + JS]
+
         keep_t = held.tile([P, PACK], F32, name="keep_t")
         nc.gpsimd.dma_start(out=keep_t[:], in_=keep.rearrange("(p t) -> p t", t=PACK))
         gain_t = held.tile([P, PACK], F32, name="gain_t")
         nc.gpsimd.dma_start(out=gain_t[:], in_=gain.rearrange("(p t) -> p t", t=PACK))
-        plane_rows(w3_s_raw, w3_scales)
+        plane_rows(nc.gpsimd, w2_s, w2_scales)
+        load_wg(nc.gpsimd, 0, 0, JS)
         b3_t = held.tile([P, 2, PACK], F32, name="b3_t")
         nc.gpsimd.dma_start(out=b3_t[:], in_=b3.rearrange("(g p t) -> p g t", g=2, t=PACK))
 
@@ -92,27 +107,18 @@ def tile_list_calving_front_retreat_kernel(
         w1_raw.append(load_w1(1))
         w2_w = held.tile([P, PASSES, 2 * H], U8, name="w2_w", align_bytes=64)
         nc.sync.dma_start(out=w2_w[:].bitcast(I32), in_=w2_words.bitcast(I32).rearrange("a p c -> p a c"))
+        w3_raw = held.tile([P, N], I32, name="w3_raw")
+        nc.sync.dma_start(out=w3_raw[:], in_=w3_words[0].rearrange("p n i -> p (n i)").bitcast(I32))
+        plane_rows(nc.sync, w3_s_raw, w3_scales)
         tab_w = [held.tile([P, T], I32, name="tab_w0"), shared.tile([P, T], I32, name="tab_w1", offset=0)]
         for a in range(PASSES):
             nc.sync.dma_start(out=tab_w[a][:], in_=tab_words[a].rearrange("p n i -> p (n i)").bitcast(I32))
         nc.sync.dma_start(list4[:], offs4)
+        nc.sync.dma_start(list2[:], offs2)
 
         page_rows = page0.rearrange("(p t) c -> t p c", t=PACK)
         page = [held.tile([P, T2], F32, name=f"page{t}") for t in range(PACK)]
         before = [page[0]] + [held.tile([P, T2], F32, name=f"before{t}") for t in range(1, PACK)]
-        wgs_rows = wgs.rearrange("(q t) j -> q t j", t=PACK)
-        wg = {}
-
-        def load_wg(u, half):
-            tile = held.tile([P, 2, HALF], F32, name=f"wg{u}{half}")
-            for quad in range(4):
-                nc.sync.dma_start(
-                    out=tile[32 * quad:32 * quad + 32, :, :],
-                    in_=wgs_rows[:, 2 * u:2 * u + 2, half * HALF:(half + 1) * HALF],
-                )
-            wg[u, half] = tile
-
-        w3_raw = held.tile([P, N], I32, name="w3_raw")
         nc.sync.dma_start(out=page[0][:], in_=page_rows[0])
         picked_s = held.tile([P, PASSES, S], U8, name="picked_s")
         for a in range(PASSES):
@@ -121,15 +127,13 @@ def tile_list_calving_front_retreat_kernel(
             nc.scalar.dma_start(
                 out=v_s[:].bitcast(I32)[r:P:32, :, :], in_=picked_s[:].bitcast(I32)[8 * r:P:32, :, :]
             )
-        nc.sync.dma_start(out=w3_raw[:], in_=w3_words[0].rearrange("p n i -> p (n i)").bitcast(I32))
-        nc.sync.dma_start(list2[:], offs2)
-        load_wg(0, 0)
         nc.sync.dma_start(out=page[1][:], in_=page_rows[1])
+        load_wg(nc.sync, 0, JS, JS)
+        load_wg(nc.sync, 0, HALF, HALF)
         nc.sync.dma_start(out=page[2][:], in_=page_rows[2])
-        load_wg(1, 0)
-        load_wg(0, 1)
+        load_wg(nc.sync, 1, 0, HALF)
         nc.sync.dma_start(out=page[3][:], in_=page_rows[3])
-        load_wg(1, 1)
+        load_wg(nc.sync, 1, HALF, HALF)
         nc.sync.dma_start(list3[:], offs3)
         for t in range(1, PACK):
             nc.sync.dma_start(out=before[t][:], in_=page_rows[t])
@@ -147,8 +151,18 @@ def tile_list_calving_front_retreat_kernel(
             w1_s.append(scales)
 
         keep_wide = held.tile([P, PACK, MW], F32, name="keep_wide")
-        for t in range(PACK):
-            nc.vector.tensor_copy(keep_wide[:, t, :], keep_t[:, t:t + 1].to_broadcast([P, MW]))
+        nc.scalar.copy(out=keep_wide[:], in_=keep_t[:].unsqueeze(2).to_broadcast([P, PACK, MW]))
+
+        w3_w = held.tile([P, N], I32, name="w3_w", align_bytes=64)
+        w3_s = held.tile([P, N], U8, name="w3_s", align_bytes=64)
+        nc.vector.tensor_copy(
+            out=w3_w[:].rearrange("p (g t c i) -> p g c t i", g=2, t=PACK, i=4),
+            in_=w3_raw[:].rearrange("p (g c i t) -> p g c t i", g=2, t=PACK, i=4),
+        )
+        nc.vector.tensor_copy(
+            out=w3_s[:].rearrange("p (g t c i) -> p g c t i", g=2, t=PACK, i=16),
+            in_=w3_s_raw[:, 0, :].rearrange("p (g c i t) -> p g c t i", g=2, t=PACK, i=16),
+        )
 
         v_w = {}
         for a in range(PASSES):
@@ -164,17 +178,6 @@ def tile_list_calving_front_retreat_kernel(
             nc.vector.tensor_tensor(
                 kept0[:, m0:m0 + MW], page[0][:].indirect(list4[:, cols(m0, MW)]), keep_wide[:, 0, :], MULT
             )
-
-        w3_w = shared.tile([P, N], I32, name="w3_w", align_bytes=64, offset=4 * M)
-        w3_s = shared.tile([P, N], U8, name="w3_s", align_bytes=64, offset=4 * M + 4 * N)
-        nc.vector.tensor_copy(
-            out=w3_w[:].rearrange("p (g t c i) -> p g c t i", g=2, t=PACK, i=4),
-            in_=w3_raw[:].rearrange("p (g c i t) -> p g c t i", g=2, t=PACK, i=4),
-        )
-        nc.vector.tensor_copy(
-            out=w3_s[:].rearrange("p (g t c i) -> p g c t i", g=2, t=PACK, i=16),
-            in_=w3_s_raw[:, 0, :].rearrange("p (g c i t) -> p g c t i", g=2, t=PACK, i=16),
-        )
 
         for j0 in range(0, S, JS):
             sums = [psum.tile([P, 2, JS], F32, name="sums", tag="turn") for u in range(2)]
@@ -207,12 +210,11 @@ def tile_list_calving_front_retreat_kernel(
                     dst = sums[t // 2][:, t % 2, jb * P:(jb + 1) * P]
                     nc.tensor.matmul(dst, lhsT=bent_sb[:, t, :], rhs=ident[:], start=True, stop=False, is_transpose=True)
                     nc.tensor.matmul(dst, lhsT=flat_sb[:, t, :], rhs=ident[:], start=False, stop=True, is_transpose=True)
-            half, c0 = divmod(j0, HALF)
             for t in range(PACK):
-                h = ring.tile([P, JS], F32, name="h", bufs=8)
+                h = ring.tile([P, JS], F32, name="h", bufs=16)
                 nc.scalar.activation(out=h[:], in_=sums[t // 2][:, t % 2, :], func=ACT.Copy, scale=gain_t[:, t:t + 1])
                 nc.vector.tensor_tensor(
-                    page[t][:].indirect(list2[:, cols(j0, JS)]), h[:], wg[t // 2, half][:, t % 2, c0:c0 + JS], MULT
+                    page[t][:].indirect(list2[:, cols(j0, JS)]), h[:], wg[t, j0], MULT
                 )
 
         y_s = held.tile([P, 2, M], U8, name="y_s", align_bytes=64)
@@ -229,7 +231,7 @@ def tile_list_calving_front_retreat_kernel(
                 old = kept0[:, m0:m0 + w] if t == 0 else kept[:, t - 1, :w]
                 nc.vector.tensor_tensor(x[:, t, :], page[t][:].indirect(list3[:, cols(m0, w)]), old, SUB)
             x_grouped = ring.tile([P, w, PACK], BF16, name="x_grouped", align_bytes=64)
-            interleave(nc.scalar.copy, x_grouped[:], x[:])
+            interleave(nc.vector.tensor_copy if m0 + w == M else nc.scalar.copy, x_grouped[:], x[:])
             x_c = ring.tile([P, w], U32, name="x_c", align_bytes=64)
             x_s = ring.tile([P, w], U8, name="x_s", align_bytes=64)
             nc.vector.quantize_mx(
@@ -271,7 +273,11 @@ def tile_list_calving_front_retreat_kernel(
             y_c = held.tile([P, 2, w], I32, name=f"y_c{index}", align_bytes=64)
             for g in range(2):
                 y_grouped = ring.tile([P, w, PACK], BF16, name=f"y_grouped{g}", align_bytes=64)
-                interleave((nc.vector.tensor_copy, nc.scalar.copy)[g], y_grouped[:], y[:, g, :, :])
+                on_vector = 0 if g == 1 else (w if index >= len(M_SLICES) - 2 else P)
+                if on_vector > 0:
+                    interleave(nc.vector.tensor_copy, y_grouped[:, :on_vector, :], y[:, g, :, :on_vector])
+                if on_vector < w:
+                    interleave(nc.scalar.copy, y_grouped[:, on_vector:, :], y[:, g, :, on_vector:])
                 nc.vector.quantize_mx(
                     out=y_c[:, g, :].bitcast(FP8X4), scales=y_s[:, g, m0:m0 + w],
                     in_=y_grouped[:].rearrange("p m t -> p (m t)"),

@@ -43,9 +43,9 @@ def tile_list_calving_front_retreat_kernel(
         shared = ctx.enter_context(tc.tile_pool(name="shared", bufs=1))
         psum = ctx.enter_context(tc.psum_pool(name="psum", bufs=4))
 
-        def plane_rows(queue, dst, src):
+        def plane_rows(dst, src):
             for r in range(4):
-                queue.dma_start(
+                nc.sync.dma_start(
                     out=dst[:].bitcast(I32)[r:P:32, :, :],
                     in_=src[:, r:16:4, :].bitcast(I32).rearrange("a q c -> q a c"),
                 )
@@ -69,10 +69,9 @@ def tile_list_calving_front_retreat_kernel(
         v_s = held.tile([P, PASSES, S], U8, name="v_s", align_bytes=64)
         w3_s_raw = held.tile([P, 1, N], U8, name="w3_s_raw")
         nc.vector.memset(tab_s[:, 0, :].bitcast(I32), 0)
-        nc.gpsimd.memset(w3_s_raw[:].bitcast(I32), 0)
-        nc.vector.memset(tab_s[:, 1, :].bitcast(I32), 0)
-        nc.gpsimd.memset(w2_s[:].bitcast(I32), 0)
-        nc.vector.memset(v_s[:].bitcast(I32), 0)
+        nc.gpsimd.memset(tab_s[:, 1, :].bitcast(I32), 0)
+        nc.vector.memset(w2_s[:].bitcast(I32), 0)
+        nc.vector.memset(w3_s_raw[:].bitcast(I32), 0)
         ident = held.tile([P, P], F32, name="ident")
         make_identity(nc, ident[:])
         warm = held.tile([P, 1], F32, name="warm")
@@ -81,60 +80,52 @@ def tile_list_calving_front_retreat_kernel(
         wgs_rows = wgs.rearrange("(q t) j -> q t j", t=PACK)
         wg = {}
 
-        def load_wg(queue, u, j0, width):
+        def load_wg(u, j0, width):
             tile = held.tile([P, 2, width], F32, name=f"wg{u}_{j0}")
             for quad in (0, 2, 1, 3):
-                queue.dma_start(
+                nc.sync.dma_start(
                     out=tile[32 * quad:32 * quad + 32, :, :], in_=wgs_rows[:, 2 * u:2 * u + 2, j0:j0 + width]
                 )
             for c0 in range(0, width, JS):
                 for tt in range(2):
                     wg[2 * u + tt, j0 + c0] = tile[:, tt, c0:c0 + JS]
 
-        keep_t = held.tile([P, PACK], F32, name="keep_t")
-        nc.gpsimd.dma_start(out=keep_t[:], in_=keep.rearrange("(p t) -> p t", t=PACK))
-        gain_t = held.tile([P, PACK], F32, name="gain_t")
-        nc.gpsimd.dma_start(out=gain_t[:], in_=gain.rearrange("(p t) -> p t", t=PACK))
-        plane_rows(nc.gpsimd, w2_s, w2_scales)
-        load_wg(nc.gpsimd, 0, 0, JS)
-        b3_t = held.tile([P, 2, PACK], F32, name="b3_t")
-        nc.gpsimd.dma_start(out=b3_t[:], in_=b3.rearrange("(g p t) -> p g t", g=2, t=PACK))
-
         w1_raw = [load_w1(0)]
-        nc.sync.dma_start(
-            out=tab_s[:].bitcast(I32)[0:P:8, :, :], in_=tab_scales.bitcast(I32).rearrange("a q c -> q a c")
-        )
+        plane_rows(tab_s, tab_scales)
         w1_raw.append(load_w1(1))
         w2_w = held.tile([P, PASSES, 2 * H], U8, name="w2_w", align_bytes=64)
         nc.sync.dma_start(out=w2_w[:].bitcast(I32), in_=w2_words.bitcast(I32).rearrange("a p c -> p a c"))
-        w3_raw = held.tile([P, N], I32, name="w3_raw")
-        nc.sync.dma_start(out=w3_raw[:], in_=w3_words[0].rearrange("p n i -> p (n i)").bitcast(I32))
-        plane_rows(nc.sync, w3_s_raw, w3_scales)
         tab_w = [held.tile([P, T], I32, name="tab_w0"), shared.tile([P, T], I32, name="tab_w1", offset=0)]
+        nc.sync.dma_start(out=tab_w[0][:], in_=tab_words[0].rearrange("p n i -> p (n i)").bitcast(I32))
+        plane_rows(w2_s, w2_scales)
+        nc.sync.dma_start(out=tab_w[1][:], in_=tab_words[1].rearrange("p n i -> p (n i)").bitcast(I32))
         for a in range(PASSES):
-            nc.sync.dma_start(out=tab_w[a][:], in_=tab_words[a].rearrange("p n i -> p (n i)").bitcast(I32))
-        nc.sync.dma_start(list4[:], offs4)
-        nc.sync.dma_start(list2[:], offs2)
+            nc.vector.tensor_copy(v_s[:, a, :], tab_s[:, a, :].indirect(list1[:]))
 
         page_rows = page0.rearrange("(p t) c -> t p c", t=PACK)
         page = [held.tile([P, T2], F32, name=f"page{t}") for t in range(PACK)]
         before = [page[0]] + [held.tile([P, T2], F32, name=f"before{t}") for t in range(1, PACK)]
+        keep_t = held.tile([P, PACK], F32, name="keep_t")
+        gain_t = held.tile([P, PACK], F32, name="gain_t")
+        b3_t = held.tile([P, 2, PACK], F32, name="b3_t")
+        w3_raw = held.tile([P, N], I32, name="w3_raw")
+        nc.sync.dma_start(list4[:], offs4)
+        nc.sync.dma_start(out=keep_t[:], in_=keep.rearrange("(p t) -> p t", t=PACK))
         nc.sync.dma_start(out=page[0][:], in_=page_rows[0])
-        picked_s = held.tile([P, PASSES, S], U8, name="picked_s")
-        for a in range(PASSES):
-            nc.vector.tensor_copy(picked_s[:, a, :], tab_s[:, a, :].indirect(list1[:]))
-        for r in range(4):
-            nc.scalar.dma_start(
-                out=v_s[:].bitcast(I32)[r:P:32, :, :], in_=picked_s[:].bitcast(I32)[8 * r:P:32, :, :]
-            )
+        nc.sync.dma_start(list2[:], offs2)
+        nc.sync.dma_start(out=gain_t[:], in_=gain.rearrange("(p t) -> p t", t=PACK))
+        nc.sync.dma_start(out=w3_raw[:], in_=w3_words[0].rearrange("p n i -> p (n i)").bitcast(I32))
+        load_wg(0, 0, JS)
         nc.sync.dma_start(out=page[1][:], in_=page_rows[1])
-        load_wg(nc.sync, 0, JS, JS)
-        load_wg(nc.sync, 0, HALF, HALF)
+        plane_rows(w3_s_raw, w3_scales)
+        load_wg(0, JS, JS)
+        load_wg(0, HALF, HALF)
         nc.sync.dma_start(out=page[2][:], in_=page_rows[2])
-        load_wg(nc.sync, 1, 0, HALF)
+        load_wg(1, 0, HALF)
         nc.sync.dma_start(out=page[3][:], in_=page_rows[3])
-        load_wg(nc.sync, 1, HALF, HALF)
+        load_wg(1, HALF, HALF)
         nc.sync.dma_start(list3[:], offs3)
+        nc.sync.dma_start(out=b3_t[:], in_=b3.rearrange("(g p t) -> p g t", g=2, t=PACK))
         for t in range(1, PACK):
             nc.sync.dma_start(out=before[t][:], in_=page_rows[t])
 
@@ -205,17 +196,18 @@ def tile_list_calving_front_retreat_kernel(
                 nc.scalar.activation(out=bent_sb[:], in_=bent[:].rearrange("j (p t) -> j t p", t=PACK), func=ACT.Tanh)
                 nc.scalar.copy(out=flat_sb[:], in_=flat[:].rearrange("j (p t) -> j t p", t=PACK))
                 parts.append((bent_sb, flat_sb))
-            for t in range(PACK):
-                for jb, (bent_sb, flat_sb) in enumerate(parts):
-                    dst = sums[t // 2][:, t % 2, jb * P:(jb + 1) * P]
-                    nc.tensor.matmul(dst, lhsT=bent_sb[:, t, :], rhs=ident[:], start=True, stop=False, is_transpose=True)
-                    nc.tensor.matmul(dst, lhsT=flat_sb[:, t, :], rhs=ident[:], start=False, stop=True, is_transpose=True)
-            for t in range(PACK):
-                h = ring.tile([P, JS], F32, name="h", bufs=16)
-                nc.scalar.activation(out=h[:], in_=sums[t // 2][:, t % 2, :], func=ACT.Copy, scale=gain_t[:, t:t + 1])
-                nc.vector.tensor_tensor(
-                    page[t][:].indirect(list2[:, cols(j0, JS)]), h[:], wg[t, j0], MULT
-                )
+            for pair in range(2):
+                for tt in range(2):
+                    t = 2 * pair + tt
+                    for jb, (bent_sb, flat_sb) in enumerate(parts):
+                        dst = sums[tt][:, pair, jb * P:(jb + 1) * P]
+                        nc.tensor.matmul(dst, lhsT=bent_sb[:, t, :], rhs=ident[:], start=True, stop=False, is_transpose=True)
+                        nc.tensor.matmul(dst, lhsT=flat_sb[:, t, :], rhs=ident[:], start=False, stop=True, is_transpose=True)
+                for tt in range(2):
+                    t = 2 * pair + tt
+                    h = ring.tile([P, JS], F32, name="h", bufs=16)
+                    nc.scalar.activation(out=h[:], in_=sums[tt][:, pair, :], func=ACT.Copy, scale=gain_t[:, t:t + 1])
+                    nc.vector.tensor_tensor(page[t][:].indirect(list2[:, cols(j0, JS)]), h[:], wg[t, j0], MULT)
 
         y_s = held.tile([P, 2, M], U8, name="y_s", align_bytes=64)
         words_out = out_1.rearrange("g p m t -> p g (m t)").bitcast(I32)

@@ -26,6 +26,9 @@ HALF = 512
 JS = 256
 M_SLICES = [(0, 128), (128, 256), (384, 256), (640, 256), (896, 128)]
 MW = 256
+H_AT = 4 * T
+H_BYTES = 4 * JS
+WG_AT = H_AT + PACK * (S // JS) * H_BYTES
 
 
 def cols(start, width):
@@ -43,9 +46,9 @@ def tile_list_calving_front_retreat_kernel(
         shared = ctx.enter_context(tc.tile_pool(name="shared", bufs=1))
         psum = ctx.enter_context(tc.psum_pool(name="psum", bufs=4))
 
-        def plane_rows(dst, src):
+        def plane_rows(queue, dst, src):
             for r in range(4):
-                nc.sync.dma_start(
+                queue.dma_start(
                     out=dst[:].bitcast(I32)[r:P:32, :, :],
                     in_=src[:, r:16:4, :].bitcast(I32).rearrange("a q c -> q a c"),
                 )
@@ -71,6 +74,7 @@ def tile_list_calving_front_retreat_kernel(
         nc.vector.memset(tab_s[:, 0, :].bitcast(I32), 0)
         nc.gpsimd.memset(tab_s[:, 1, :].bitcast(I32), 0)
         nc.vector.memset(w2_s[:].bitcast(I32), 0)
+        nc.vector.memset(v_s[:].bitcast(I32), 0)
         nc.vector.memset(w3_s_raw[:].bitcast(I32), 0)
         ident = held.tile([P, P], F32, name="ident")
         make_identity(nc, ident[:])
@@ -81,7 +85,10 @@ def tile_list_calving_front_retreat_kernel(
         wg = {}
 
         def load_wg(u, j0, width):
-            tile = held.tile([P, 2, width], F32, name=f"wg{u}_{j0}")
+            if (u, j0) == (0, HALF):
+                tile = shared.tile([P, 2, width], F32, name=f"wg{u}_{j0}", offset=WG_AT)
+            else:
+                tile = held.tile([P, 2, width], F32, name=f"wg{u}_{j0}")
             for quad in (0, 2, 1, 3):
                 nc.sync.dma_start(
                     out=tile[32 * quad:32 * quad + 32, :, :], in_=wgs_rows[:, 2 * u:2 * u + 2, j0:j0 + width]
@@ -90,17 +97,24 @@ def tile_list_calving_front_retreat_kernel(
                 for tt in range(2):
                     wg[2 * u + tt, j0 + c0] = tile[:, tt, c0:c0 + JS]
 
+        plane_rows(nc.gpsimd, w2_s, w2_scales)
         w1_raw = [load_w1(0)]
-        plane_rows(tab_s, tab_scales)
+        nc.sync.dma_start(
+            out=tab_s[:].bitcast(I32)[4:P:8, :, :], in_=tab_scales.bitcast(I32).rearrange("a q c -> q a c")
+        )
         w1_raw.append(load_w1(1))
         w2_w = held.tile([P, PASSES, 2 * H], U8, name="w2_w", align_bytes=64)
         nc.sync.dma_start(out=w2_w[:].bitcast(I32), in_=w2_words.bitcast(I32).rearrange("a p c -> p a c"))
         tab_w = [held.tile([P, T], I32, name="tab_w0"), shared.tile([P, T], I32, name="tab_w1", offset=0)]
         nc.sync.dma_start(out=tab_w[0][:], in_=tab_words[0].rearrange("p n i -> p (n i)").bitcast(I32))
-        plane_rows(w2_s, w2_scales)
         nc.sync.dma_start(out=tab_w[1][:], in_=tab_words[1].rearrange("p n i -> p (n i)").bitcast(I32))
+        picked_s = held.tile([P, PASSES, S], U8, name="picked_s")
         for a in range(PASSES):
-            nc.vector.tensor_copy(v_s[:, a, :], tab_s[:, a, :].indirect(list1[:]))
+            nc.vector.tensor_copy(picked_s[:, a, :], tab_s[:, a, :].indirect(list1[:]))
+        for r in range(4):
+            nc.gpsimd.dma_start(
+                out=v_s[:].bitcast(I32)[r:P:32, :, :], in_=picked_s[:].bitcast(I32)[8 * r + 4:P:32, :, :]
+            )
 
         page_rows = page0.rearrange("(p t) c -> t p c", t=PACK)
         page = [held.tile([P, T2], F32, name=f"page{t}") for t in range(PACK)]
@@ -114,18 +128,18 @@ def tile_list_calving_front_retreat_kernel(
         nc.sync.dma_start(out=page[0][:], in_=page_rows[0])
         nc.sync.dma_start(list2[:], offs2)
         nc.sync.dma_start(out=gain_t[:], in_=gain.rearrange("(p t) -> p t", t=PACK))
-        nc.sync.dma_start(out=w3_raw[:], in_=w3_words[0].rearrange("p n i -> p (n i)").bitcast(I32))
         load_wg(0, 0, JS)
         nc.sync.dma_start(out=page[1][:], in_=page_rows[1])
-        plane_rows(w3_s_raw, w3_scales)
-        load_wg(0, JS, JS)
-        load_wg(0, HALF, HALF)
         nc.sync.dma_start(out=page[2][:], in_=page_rows[2])
-        load_wg(1, 0, HALF)
+        load_wg(1, 0, JS)
         nc.sync.dma_start(out=page[3][:], in_=page_rows[3])
-        load_wg(1, HALF, HALF)
+        for j0, width in ((JS, JS), (HALF, HALF)):
+            for u in range(2):
+                load_wg(u, j0, width)
         nc.sync.dma_start(list3[:], offs3)
         nc.sync.dma_start(out=b3_t[:], in_=b3.rearrange("(g p t) -> p g t", g=2, t=PACK))
+        nc.sync.dma_start(out=w3_raw[:], in_=w3_words[0].rearrange("p n i -> p (n i)").bitcast(I32))
+        plane_rows(nc.sync, w3_s_raw, w3_scales)
         for t in range(1, PACK):
             nc.sync.dma_start(out=before[t][:], in_=page_rows[t])
 
@@ -144,17 +158,6 @@ def tile_list_calving_front_retreat_kernel(
         keep_wide = held.tile([P, PACK, MW], F32, name="keep_wide")
         nc.scalar.copy(out=keep_wide[:], in_=keep_t[:].unsqueeze(2).to_broadcast([P, PACK, MW]))
 
-        w3_w = held.tile([P, N], I32, name="w3_w", align_bytes=64)
-        w3_s = held.tile([P, N], U8, name="w3_s", align_bytes=64)
-        nc.vector.tensor_copy(
-            out=w3_w[:].rearrange("p (g t c i) -> p g c t i", g=2, t=PACK, i=4),
-            in_=w3_raw[:].rearrange("p (g c i t) -> p g c t i", g=2, t=PACK, i=4),
-        )
-        nc.vector.tensor_copy(
-            out=w3_s[:].rearrange("p (g t c i) -> p g c t i", g=2, t=PACK, i=16),
-            in_=w3_s_raw[:, 0, :].rearrange("p (g c i t) -> p g c t i", g=2, t=PACK, i=16),
-        )
-
         v_w = {}
         for a in range(PASSES):
             for half in range(S // HALF):
@@ -172,29 +175,28 @@ def tile_list_calving_front_retreat_kernel(
 
         for j0 in range(0, S, JS):
             sums = [psum.tile([P, 2, JS], F32, name="sums", tag="turn") for u in range(2)]
+            blocks = range(j0, j0 + JS, P)
+            bent = {j: psum.tile([P, H], F32, name="bent", tag="prod") for j in blocks}
+            flat = {j: psum.tile([P, H], F32, name="flat", tag="prod") for j in blocks}
+            for a in range(PASSES):
+                for j in blocks:
+                    half, c0 = divmod(j, HALF)
+                    for acc, words, scales in (
+                        (bent[j], w2_w[:, a, :].bitcast(FP4X4), w2_s[:, a, :]),
+                        (flat[j], w1_c[a][:].bitcast(FP8X4), w1_s[a][:]),
+                    ):
+                        nc.tensor.matmul_mx(
+                            out=acc[:],
+                            lhsT=v_w[a, half][:, c0:c0 + P].bitcast(FP8X4), lhsT_scale=v_s[:, a, j:j + P],
+                            rhs=words, rhs_scale=scales,
+                            start=(a == 0), stop=(a == PASSES - 1),
+                        )
             parts = []
-            for jb in range(JS // P):
-                j = j0 + jb * P
-                half, c0 = divmod(j, HALF)
-                flat = psum.tile([P, H], F32, name="flat", tag="prod")
-                bent = psum.tile([P, H], F32, name="bent", tag="prod")
-                for a in range(PASSES):
-                    nc.tensor.matmul_mx(
-                        out=bent[:],
-                        lhsT=v_w[a, half][:, c0:c0 + P].bitcast(FP8X4), lhsT_scale=v_s[:, a, j:j + P],
-                        rhs=w2_w[:, a, :].bitcast(FP4X4), rhs_scale=w2_s[:, a, :],
-                        start=(a == 0), stop=(a == PASSES - 1),
-                    )
-                    nc.tensor.matmul_mx(
-                        out=flat[:],
-                        lhsT=v_w[a, half][:, c0:c0 + P].bitcast(FP8X4), lhsT_scale=v_s[:, a, j:j + P],
-                        rhs=w1_c[a][:].bitcast(FP8X4), rhs_scale=w1_s[a][:],
-                        start=(a == 0), stop=(a == PASSES - 1),
-                    )
+            for j in blocks:
                 bent_sb = ring.tile([P, PACK, P], F32, name="bent_sb", bufs=3)
                 flat_sb = ring.tile([P, PACK, P], F32, name="flat_sb", bufs=3)
-                nc.scalar.activation(out=bent_sb[:], in_=bent[:].rearrange("j (p t) -> j t p", t=PACK), func=ACT.Tanh)
-                nc.scalar.copy(out=flat_sb[:], in_=flat[:].rearrange("j (p t) -> j t p", t=PACK))
+                nc.scalar.activation(out=bent_sb[:], in_=bent[j][:].rearrange("j (p t) -> j t p", t=PACK), func=ACT.Tanh)
+                nc.scalar.copy(out=flat_sb[:], in_=flat[j][:].rearrange("j (p t) -> j t p", t=PACK))
                 parts.append((bent_sb, flat_sb))
             for pair in range(2):
                 for tt in range(2):
@@ -205,15 +207,26 @@ def tile_list_calving_front_retreat_kernel(
                         nc.tensor.matmul(dst, lhsT=flat_sb[:, t, :], rhs=ident[:], start=False, stop=True, is_transpose=True)
                 for tt in range(2):
                     t = 2 * pair + tt
-                    h = ring.tile([P, JS], F32, name="h", bufs=16)
+                    h = shared.tile([P, JS], F32, name=f"h{t}_{j0}", offset=H_AT + (j0 // JS * PACK + t) * H_BYTES)
                     nc.scalar.activation(out=h[:], in_=sums[tt][:, pair, :], func=ACT.Copy, scale=gain_t[:, t:t + 1])
                     nc.vector.tensor_tensor(page[t][:].indirect(list2[:, cols(j0, JS)]), h[:], wg[t, j0], MULT)
+
+        w3_w = shared.tile([P, N], I32, name="w3_w", align_bytes=64, offset=H_AT + 2 * PACK * H_BYTES)
+        w3_s = shared.tile([P, N], U8, name="w3_s", align_bytes=64, offset=H_AT + 3 * PACK * H_BYTES)
+        nc.vector.tensor_copy(
+            out=w3_w[:].rearrange("p (g t c i) -> p g c t i", g=2, t=PACK, i=4),
+            in_=w3_raw[:].rearrange("p (g c i t) -> p g c t i", g=2, t=PACK, i=4),
+        )
+        nc.vector.tensor_copy(
+            out=w3_s[:].rearrange("p (g t c i) -> p g c t i", g=2, t=PACK, i=16),
+            in_=w3_s_raw[:, 0, :].rearrange("p (g c i t) -> p g c t i", g=2, t=PACK, i=16),
+        )
 
         y_s = held.tile([P, 2, M], U8, name="y_s", align_bytes=64)
         words_out = out_1.rearrange("g p m t -> p g (m t)").bitcast(I32)
 
         def gather_x(m0, w):
-            kept = ring.tile([P, PACK - 1, MW], F32, name="kept", bufs=1)
+            kept = shared.tile([P, PACK - 1, MW], F32, name="kept", offset=WG_AT)
             for t in range(1, PACK):
                 nc.vector.tensor_tensor(
                     kept[:, t - 1, :w], before[t][:].indirect(list4[:, cols(m0, w)]), keep_wide[:, t, :w], MULT

from contextlib import ExitStack

import concourse.mybir as mybir
from concourse.masks import make_identity

K, T, S, H, T2, M, N = 1024, 4096, 1024, 512, 2048, 1024, 1024
FLOPS = 2 * (2 * K * H * S + H * N * M)

F32 = mybir.dt.float32
BF16 = mybir.dt.bfloat16
I32 = mybir.dt.int32
U32 = mybir.dt.uint32
U16 = mybir.dt.uint16
U8 = mybir.dt.uint8
FP8X4 = mybir.dt.float8_e4m3fn_x4
FP4X4 = mybir.dt.float4_e2m1fn_x4
ACT = mybir.ActivationFunctionType
MULT = mybir.AluOpType.mult
SUB = mybir.AluOpType.subtract
ADD = mybir.AluOpType.add

P = 128
PACK = 4
PASSES = K // (P * PACK)
HALF = 512
JS = 256
M_SLICES = [(0, 128), (128, 256), (384, 256), (640, 256), (896, 128)]
MW = 256
H_AT = 4 * T
H_BYTES = 4 * JS
WG_AT = H_AT + PACK * (S // JS) * H_BYTES


def cols(start, width):
    return slice(start // 16, (start + width) // 16)


def tile_list_calving_front_retreat_kernel(
    tc, tab_words, tab_scales, offs, w1, w2_words, w2_scales, gain, page0, wgs, offs2, offs3, offs4, keep,
    w3_words, w3_scales, b3, out_0, out_1, out_2,
):
    nc = tc.nc
    with ExitStack() as ctx:
        held = ctx.enter_context(tc.tile_pool(name="held", bufs=1))
        ring = ctx.enter_context(tc.tile_pool(name="ring", bufs=2))
        shared = ctx.enter_context(tc.tile_pool(name="shared", bufs=1))
        psum = ctx.enter_context(tc.psum_pool(name="psum", bufs=4))

        def plane_rows(queue, dst, src):
            for r in range(4):
                queue.dma_start(
                    out=dst[:].bitcast(I32)[r:P:32, :, :],
                    in_=src[:, r:16:4, :].bitcast(I32).rearrange("a q c -> q a c"),
                )

        def interleave(copy, dst, src):
            copy(out=dst.rearrange("p (c i) t -> p c t i", i=4), in_=src.rearrange("p t (c i) -> p c t i", i=4))

        list1 = held.tile([P, S // 16], U16, name="list1")
        list2 = held.tile([P, S // 16], U16, name="list2")
        list3 = held.tile([P, M // 16], U16, name="list3")
        list4 = held.tile([P, M // 16], U16, name="list4")
        nc.sync.dma_start(list1[:], offs)

        def load_w1(a):
            raw = ring.tile([P, PACK, H], F32, name="w1_raw", tag="wide")
            nc.sync.dma_start(out=raw[:], in_=w1[a * 512:(a + 1) * 512, :].rearrange("(p i) r -> p i r", i=PACK))
            return raw

        tab_s = held.tile([P, PASSES, T], U8, name="tab_s")
        w2_s = held.tile([P, PASSES, H], U8, name="w2_s", align_bytes=64)
        v_s = held.tile([P, PASSES, S], U8, name="v_s", align_bytes=64)
        w3_s_raw = held.tile([P, 1, N], U8, name="w3_s_raw")
        nc.vector.memset(tab_s[:, 0, :].bitcast(I32), 0)
        nc.gpsimd.memset(tab_s[:, 1, :].bitcast(I32), 0)
        nc.vector.memset(w2_s[:].bitcast(I32), 0)
        nc.vector.memset(v_s[:].bitcast(I32), 0)
        nc.vector.memset(w3_s_raw[:].bitcast(I32), 0)
        ident = held.tile([P, P], F32, name="ident")
        make_identity(nc, ident[:])
        warm = held.tile([P, 1], F32, name="warm")
        nc.scalar.activation(out=warm[:], in_=ident[:, 0:1], func=ACT.Tanh)

        wgs_rows = wgs.rearrange("(q t) j -> q t j", t=PACK)
        wg = {}

        def load_wg(u, j0, width):
            if (u, j0) == (0, HALF):
                tile = shared.tile([P, 2, width], F32, name=f"wg{u}_{j0}", offset=WG_AT)
            else:
                tile = held.tile([P, 2, width], F32, name=f"wg{u}_{j0}")
            for quad in (0, 2, 1, 3):
                nc.sync.dma_start(
                    out=tile[32 * quad:32 * quad + 32, :, :], in_=wgs_rows[:, 2 * u:2 * u + 2, j0:j0 + width]
                )
            for c0 in range(0, width, JS):
                for tt in range(2):
                    wg[2 * u + tt, j0 + c0] = tile[:, tt, c0:c0 + JS]

        plane_rows(nc.gpsimd, w2_s, w2_scales)
        w1_raw = [load_w1(0)]
        nc.sync.dma_start(
            out=tab_s[:].bitcast(I32)[4:P:8, :, :], in_=tab_scales.bitcast(I32).rearrange("a q c -> q a c")
        )
        w1_raw.append(load_w1(1))
        w2_w = held.tile([P, PASSES, 2 * H], U8, name="w2_w", align_bytes=64)
        nc.sync.dma_start(out=w2_w[:].bitcast(I32), in_=w2_words.bitcast(I32).rearrange("a p c -> p a c"))
        tab_w = [held.tile([P, T], I32, name="tab_w0"), shared.tile([P, T], I32, name="tab_w1", offset=0)]
        nc.sync.dma_start(out=tab_w[0][:], in_=tab_words[0].rearrange("p n i -> p (n i)").bitcast(I32))
        nc.sync.dma_start(out=tab_w[1][:], in_=tab_words[1].rearrange("p n i -> p (n i)").bitcast(I32))
        picked_s = held.tile([P, PASSES, S], U8, name="picked_s")
        for a in range(PASSES):
            nc.vector.tensor_copy(picked_s[:, a, :], tab_s[:, a, :].indirect(list1[:]))
        for r in range(4):
            nc.gpsimd.dma_start(
                out=v_s[:].bitcast(I32)[r:P:32, :, :], in_=picked_s[:].bitcast(I32)[8 * r + 4:P:32, :, :]
            )

        page_rows = page0.rearrange("(p t) c -> t p c", t=PACK)
        page = [held.tile([P, T2], F32, name=f"page{t}") for t in range(PACK)]
        before = [page[0]] + [held.tile([P, T2], F32, name=f"before{t}") for t in range(1, PACK)]
        keep_t = held.tile([P, PACK], F32, name="keep_t")
        gain_t = held.tile([P, PACK], F32, name="gain_t")
        b3_t = held.tile([P, 2, PACK], F32, name="b3_t")
        w3_raw = held.tile([P, N], I32, name="w3_raw")
        nc.sync.dma_start(list4[:], offs4)
        nc.sync.dma_start(out=keep_t[:], in_=keep.rearrange("(p t) -> p t", t=PACK))
        nc.sync.dma_start(out=page[0][:], in_=page_rows[0])
        nc.sync.dma_start(list2[:], offs2)
        nc.sync.dma_start(out=gain_t[:], in_=gain.rearrange("(p t) -> p t", t=PACK))
        load_wg(0, 0, JS)
        nc.sync.dma_start(out=page[1][:], in_=page_rows[1])
        nc.sync.dma_start(out=page[2][:], in_=page_rows[2])
        load_wg(1, 0, JS)
        nc.sync.dma_start(out=page[3][:], in_=page_rows[3])
        for j0, width in ((JS, JS), (HALF, HALF)):
            for u in range(2):
                load_wg(u, j0, width)
        nc.sync.dma_start(list3[:], offs3)
        nc.sync.dma_start(out=b3_t[:], in_=b3.rearrange("(g p t) -> p g t", g=2, t=PACK))
        nc.sync.dma_start(out=w3_raw[:], in_=w3_words[0].rearrange("p n i -> p (n i)").bitcast(I32))
        plane_rows(nc.sync, w3_s_raw, w3_scales)
        for t in range(1, PACK):
            nc.sync.dma_start(out=before[t][:], in_=page_rows[t])

        w1_c, w1_s = [], []
        for a in range(PASSES):
            grouped = ring.tile([P, H, PACK], BF16, name="w1_grouped", align_bytes=64)
            interleave(nc.scalar.copy, grouped[:], w1_raw[a][:])
            codes = held.tile([P, H], U32, name=f"w1_c{a}", align_bytes=64)
            scales = held.tile([P, H], U8, name=f"w1_s{a}", align_bytes=64)
            nc.vector.quantize_mx(
                out=codes[:].bitcast(FP8X4), scales=scales[:], in_=grouped[:].rearrange("p r i -> p (r i)")
            )
            w1_c.append(codes)
            w1_s.append(scales)

        keep_wide = held.tile([P, PACK, MW], F32, name="keep_wide")
        nc.scalar.copy(out=keep_wide[:], in_=keep_t[:].unsqueeze(2).to_broadcast([P, PACK, MW]))

        v_w = {}
        for a in range(PASSES):
            for half in range(S // HALF):
                picked = held.tile([P, HALF], U32, name=f"v_w{a}{half}", align_bytes=64)
                nc.vector.tensor_copy(
                    picked[:], tab_w[a][:].bitcast(U32).indirect(list1[:, cols(half * HALF, HALF)])
                )
                v_w[a, half] = picked

        kept0 = shared.tile([P, M], F32, name="kept0", offset=0)
        for m0 in range(0, M, MW):
            nc.vector.tensor_tensor(
                kept0[:, m0:m0 + MW], page[0][:].indirect(list4[:, cols(m0, MW)]), keep_wide[:, 0, :], MULT
            )

        for j0 in range(0, S, JS):
            sums = [psum.tile([P, 2, JS], F32, name="sums", tag="turn") for u in range(2)]
            blocks = range(j0, j0 + JS, P)
            bent = {j: psum.tile([P, H], F32, name="bent", tag="prod") for j in blocks}
            flat = {j: psum.tile([P, H], F32, name="flat", tag="prod") for j in blocks}
            for a in range(PASSES):
                for j in blocks:
                    half, c0 = divmod(j, HALF)
                    for acc, words, scales in (
                        (bent[j], w2_w[:, a, :].bitcast(FP4X4), w2_s[:, a, :]),
                        (flat[j], w1_c[a][:].bitcast(FP8X4), w1_s[a][:]),
                    ):
                        nc.tensor.matmul_mx(
                            out=acc[:],
                            lhsT=v_w[a, half][:, c0:c0 + P].bitcast(FP8X4), lhsT_scale=v_s[:, a, j:j + P],
                            rhs=words, rhs_scale=scales,
                            start=(a == 0), stop=(a == PASSES - 1),
                        )
            parts = []
            for j in blocks:
                bent_sb = ring.tile([P, PACK, P], F32, name="bent_sb", bufs=3)
                flat_sb = ring.tile([P, PACK, P], F32, name="flat_sb", bufs=3)
                nc.scalar.activation(out=bent_sb[:], in_=bent[j][:].rearrange("j (p t) -> j t p", t=PACK), func=ACT.Tanh)
                nc.scalar.copy(out=flat_sb[:], in_=flat[j][:].rearrange("j (p t) -> j t p", t=PACK))
                parts.append((bent_sb, flat_sb))
            for pair in range(2):
                for tt in range(2):
                    t = 2 * pair + tt
                    for jb, (bent_sb, flat_sb) in enumerate(parts):
                        dst = sums[tt][:, pair, jb * P:(jb + 1) * P]
                        nc.tensor.matmul(dst, lhsT=bent_sb[:, t, :], rhs=ident[:], start=True, stop=False, is_transpose=True)
                        nc.tensor.matmul(dst, lhsT=flat_sb[:, t, :], rhs=ident[:], start=False, stop=True, is_transpose=True)
                for tt in range(2):
                    t = 2 * pair + tt
                    h = shared.tile([P, JS], F32, name=f"h{t}_{j0}", offset=H_AT + (j0 // JS * PACK + t) * H_BYTES)
                    nc.scalar.activation(out=h[:], in_=sums[tt][:, pair, :], func=ACT.Copy, scale=gain_t[:, t:t + 1])
                    nc.vector.tensor_tensor(page[t][:].indirect(list2[:, cols(j0, JS)]), h[:], wg[t, j0], MULT)

        w3_w = shared.tile([P, N], I32, name="w3_w", align_bytes=64, offset=H_AT + 2 * PACK * H_BYTES)
        w3_s = shared.tile([P, N], U8, name="w3_s", align_bytes=64, offset=H_AT + 3 * PACK * H_BYTES)
        nc.vector.tensor_copy(
            out=w3_w[:].rearrange("p (g t c i) -> p g c t i", g=2, t=PACK, i=4),
            in_=w3_raw[:].rearrange("p (g c i t) -> p g c t i", g=2, t=PACK, i=4),
        )
        nc.vector.tensor_copy(
            out=w3_s[:].rearrange("p (g t c i) -> p g c t i", g=2, t=PACK, i=16),
            in_=w3_s_raw[:, 0, :].rearrange("p (g c i t) -> p g c t i", g=2, t=PACK, i=16),
        )

        y_s = held.tile([P, 2, M], U8, name="y_s", align_bytes=64)
        words_out = out_1.rearrange("g p m t -> p g (m t)").bitcast(I32)

        def gather_x(m0, w):
            kept = shared.tile([P, PACK - 1, MW], F32, name="kept", offset=WG_AT)
            for t in range(1, PACK):
                nc.vector.tensor_tensor(
                    kept[:, t - 1, :w], before[t][:].indirect(list4[:, cols(m0, w)]), keep_wide[:, t, :w], MULT
                )
            x = ring.tile([P, PACK, w], F32, name="x", bufs=1)
            for t in range(PACK):
                old = kept0[:, m0:m0 + w] if t == 0 else kept[:, t - 1, :w]
                nc.vector.tensor_tensor(x[:, t, :], page[t][:].indirect(list3[:, cols(m0, w)]), old, SUB)
            x_grouped = ring.tile([P, w, PACK], BF16, name="x_grouped", align_bytes=64)
            interleave(nc.vector.tensor_copy if m0 + w == M else nc.scalar.copy, x_grouped[:], x[:])
            x_c = ring.tile([P, w], U32, name="x_c", align_bytes=64)
            x_s = ring.tile([P, w], U8, name="x_s", align_bytes=64)
            nc.vector.quantize_mx(
                out=x_c[:].bitcast(FP8X4), scales=x_s[:], in_=x_grouped[:].rearrange("p m t -> p (m t)")
            )
            return x_c, x_s

        def multiply(index, x_c, x_s):
            m0, w = M_SLICES[index]
            per_bank = 512 // w
            y = ring.tile([P, 2, PACK, w], F32, name="y", tag="wide")
            for g in range(2):
                for t0 in range(0, PACK, per_bank):
                    bank = psum.tile([P, per_bank, w], F32, name="bank", tag=("prod", "turn")[index % 2])
                    for tt in range(per_bank):
                        c0 = (g * PACK + t0 + tt) * P
                        nc.tensor.matmul_mx(
                            out=bank[:, tt, :],
                            lhsT=w3_w[:, c0:c0 + P].bitcast(FP8X4), lhsT_scale=w3_s[:, c0:c0 + P],
                            rhs=x_c[:].bitcast(FP8X4), rhs_scale=x_s[:],
                            start=True, stop=True,
                        )
                    if index == len(M_SLICES) - 1 and g == 0:
                        bias = b3_t[:, g, t0:t0 + per_bank].unsqueeze(2).to_broadcast([P, per_bank, w])
                        nc.vector.tensor_tensor(y[:, g, t0:t0 + per_bank, :], bank[:], bias, ADD)
                    else:
                        for tt in range(per_bank):
                            t = t0 + tt
                            nc.scalar.activation(
                                out=y[:, g, t, :], in_=bank[:, tt, :], func=ACT.Identity, bias=b3_t[:, g, t:t + 1]
                            )
                nc.sync.dma_start(
                    out=out_0[g * 512:(g + 1) * 512, m0:m0 + w].rearrange("(p t) m -> p t m", t=PACK), in_=y[:, g, :, :]
                )
            return y

        def planes(index, y):
            m0, w = M_SLICES[index]
            y_c = held.tile([P, 2, w], I32, name=f"y_c{index}", align_bytes=64)
            for g in range(2):
                y_grouped = ring.tile([P, w, PACK], BF16, name=f"y_grouped{g}", align_bytes=64)
                on_vector = 0 if g == 1 else (w if index >= len(M_SLICES) - 2 else P)
                if on_vector > 0:
                    interleave(nc.vector.tensor_copy, y_grouped[:, :on_vector, :], y[:, g, :, :on_vector])
                if on_vector < w:
                    interleave(nc.scalar.copy, y_grouped[:, on_vector:, :], y[:, g, :, on_vector:])
                nc.vector.quantize_mx(
                    out=y_c[:, g, :].bitcast(FP8X4), scales=y_s[:, g, m0:m0 + w],
                    in_=y_grouped[:].rearrange("p m t -> p (m t)"),
                )
            nc.sync.dma_start(out=words_out[:, :, m0:m0 + w], in_=y_c[:])

        quantised = gather_x(*M_SLICES[0])
        for index in range(len(M_SLICES)):
            y = multiply(index, *quantised)
            if index + 1 < len(M_SLICES):
                quantised = gather_x(*M_SLICES[index + 1])
            planes(index, y)
        for r in range(4):
            nc.scalar.dma_start(
                out=out_2[:, r:16:4, :].bitcast(I32).rearrange("g q m -> q g m"),
                in_=y_s[:].bitcast(I32)[r:P:32, :, :],
            )
